import numpy as np
import ml_dtypes


def mxq(x, axis, fmt="e4m3"):
    dtype, down = {"e4m3": (ml_dtypes.float8_e4m3fn, 7), "e5m2": (ml_dtypes.float8_e5m2, 14)}[fmt]
    v = np.moveaxis(np.asarray(x, np.float32).astype(ml_dtypes.bfloat16).astype(np.float64), axis, -1)
    blocks = v.reshape(v.shape[:-1] + (-1, 32))
    amax = np.abs(blocks).max(-1, keepdims=True)
    byte = np.maximum(np.where(amax > 0, np.frexp(amax)[1] - 1 + 127, 0) - down, 1)
    scale = np.exp2(byte - 127.0)
    codes = (blocks / scale).astype(np.float32).astype(dtype).astype(np.float64)
    return np.moveaxis((codes * scale).reshape(v.shape), -1, axis)


WIDE = False


def mx_kscale(k):
    if not WIDE:
        return np.ones(k)
    levels = np.array([30, -30])
    if k % 512:
        return np.exp2(np.random.permutation(np.resize(levels, k // 32))).repeat(32)
    a = np.empty((k // 512, 16))
    for p in range(k // 512):
        a[p, :8] = np.random.permutation(np.resize(levels, 8))
        for g in range(8):
            far = levels[np.abs(levels - a[p, g]) >= 10]
            a[p, g + 8] = far[np.random.randint(len(far))]
    return np.exp2(a.ravel()).repeat(32)


def f64(x):
    return np.asarray(x).astype(np.float64)


def striped(idx):
    return np.tile(np.asarray(idx).reshape(-1, 16).T, (8, 1)).astype(np.uint16)


def unstriped(offs):
    return offs[:16].T.reshape(-1).astype(np.int64)


E2M1 = np.array([0.0, 0.5, 1.0, 1.5, 2.0, 3.0, 4.0, 6.0, -0.0, -0.5, -1.0, -1.5, -2.0, -3.0, -4.0, -6.0])


def pack_weight(w, fmt):
    k, n = w.shape
    w = f64(np.asarray(w, np.float32).astype(ml_dtypes.bfloat16)).reshape(k // 32, 32, n)
    amax = np.abs(w).max(1)
    if fmt == "e4m3":
        byte = np.frexp(amax)[1] - 1 + 127 - 7
    else:
        mant, ex = np.frexp(amax / 6.0)
        byte = np.where(mant > 0.5, ex, ex - 1) + 127
    byte = np.clip(np.where(amax > 0, byte, 1), 1, 254)
    scaled = (w * np.exp2(127.0 - byte)[:, None, :]).reshape(k, n).astype(np.float32)
    by_word = np.ascontiguousarray(scaled.reshape(k // 512, 128, 4, n).transpose(0, 1, 3, 2))
    if fmt == "e4m3":
        words = by_word.astype(ml_dtypes.float8_e4m3fn).view(np.uint8)
    else:
        c = by_word.astype(ml_dtypes.float4_e2m1fn).view(np.uint8) & 0xF
        words = (c[..., 0::2] | (c[..., 1::2] << 4)).reshape(k // 512, 128, 2 * n)
    return np.ascontiguousarray(words), np.ascontiguousarray(byte.astype(np.uint8).reshape(k // 512, 16, n))


def unpack_weight(words, scales, fmt):
    g, _, n = scales.shape
    words = np.ascontiguousarray(words).reshape(g, 128, n, -1)
    if fmt == "e4m3":
        vals = words.view(ml_dtypes.float8_e4m3fn).astype(np.float64)
    else:
        nib = np.empty((g, 128, n, 4), np.uint8)
        nib[..., 0::2] = words & 0xF
        nib[..., 1::2] = words >> 4
        vals = E2M1[nib]
    vals = vals * np.repeat(np.exp2(scales.astype(np.float64) - 127.0), 8, axis=1)[..., None]
    return vals.transpose(0, 1, 3, 2).reshape(g * 512, n)


K, T, J, I, S, V = 1024, 1024, 256, 256, 512, 1024


def setup_inputs():
    n = np.random.standard_normal
    idx = np.random.permutation(T)[:J]
    idx2 = np.random.permutation(S)[:J]
    idx3 = np.random.permutation(V)[:I]
    fk = mx_kscale(K)
    kyp = pack_weight(n((K, V)) / fk[:, None], "e2m1")
    return {
        "xf": (n((K, T)) * 0.03).astype(np.float32),
        "xb": (n((K, S))).astype(np.float32),
        "fk": (np.random.uniform(0.5, 2.0, (K, 1)) * fk[:, None]).astype(np.float32),
        "ky_words": kyp[0],
        "ky_scales": kyp[1],
        "bi": (np.random.uniform(-0.7, 0.7, (1, I))).astype(np.float32),
        "tg": (np.random.uniform(-0.5, 1.5, (J, 1))).astype(np.float32),
        "offs": striped(idx),
        "offs2": striped(idx2),
        "offs3": striped(idx3),
    }


def reference(xf, xb, fk, ky_words, ky_scales, bi, tg, offs, offs2, offs3):
    idx = unstriped(offs)
    idx2 = unstriped(offs2)
    idx3 = unstriped(offs3)
    kyu = unpack_weight(ky_words, ky_scales, "e2m1")
    u = f64(xf)[:, idx] * f64(xb)[:, idx2] * f64(fk)
    uq = mxq(u, 0, "e5m2")
    kyidx3g = kyu[:, idx3]
    a0 = uq.T @ kyidx3g
    a = a0 + f64(bi)
    y = np.square(np.maximum(a - f64(tg), 0.0))
    return y

@@ -1,0 +1,200 @@
+from contextlib import ExitStack
+
+import concourse.mybir as mybir
+from concourse.masks import make_identity
+
+K, T, J, I, S, V = 1024, 1024, 256, 256, 512, 1024
+FLOPS = 2 * K * J * I
+
+F32 = mybir.dt.float32
+BF16 = mybir.dt.bfloat16
+I32 = mybir.dt.int32
+U32 = mybir.dt.uint32
+U16 = mybir.dt.uint16
+U8 = mybir.dt.uint8
+E5M2X4 = mybir.dt.float8_e5m2_x4
+E2M1X4 = mybir.dt.float4_e2m1fn_x4
+ALU = mybir.AluOpType
+ACT = mybir.ActivationFunctionType
+
+P = 128
+PACK = 4
+PASSES = K // (P * PACK)
+HALVES = J // P
+
+
+def tile_list_scores_products_listed_hinge_kernel(tc, xf, xb, fk, ky_words, ky_scales, bi, tg, offs, offs2, offs3, out):
+    nc = tc.nc
+    with ExitStack() as ctx:
+        keep = ctx.enter_context(tc.tile_pool(name="keep", bufs=1))
+        psum = ctx.enter_context(tc.psum_pool(name="psum", bufs=1))
+
+        list_f = keep.tile([P, J // 16], U16, name="list_f")
+        list_b = keep.tile([P, J // 16], U16, name="list_b")
+        list_k = keep.tile([P, I // 16], U16, name="list_k")
+
+        xf_planes = xf.rearrange("(a p t) w -> a p t w", a=PASSES, t=PACK)
+        xb_planes = xb.rearrange("(a p t) w -> a p t w", a=PASSES, t=PACK)
+        xf_window, xb_window = {}, {}
+
+        def load_planes(windows, planes, label, a, first, count):
+            width = planes.shape[3]
+            tile = keep.tile([P, count * width], F32, name=f"{label}_{a}_{first}")
+            nc.sync.dma_start(out=tile[:], in_=planes[a][:, first : first + count, :].rearrange("p t w -> p (t w)"))
+            for t in range(count):
+                windows[a, first + t] = tile[:, t * width : (t + 1) * width]
+
+        rows = keep.tile([P, P * PACK], F32, name="rows")
+        nc.vector.memset(rows[:], 0.0)
+        short_rows = keep.tile([P, P], F32, name="short_rows")
+        nc.vector.memset(short_rows[:], 0.0)
+        key_scales = keep.tile([P, PASSES * V], U8, name="key_scales", align_bytes=64)
+        nc.vector.memset(key_scales[:].bitcast(I32), 0)
+        key_words = [keep.tile([P, V], U16, name=f"key_words_{a}", align_bytes=64) for a in range(PASSES)]
+
+        def load_scales(q):
+            nc.sync.dma_start(
+                out=key_scales[32 * q : 32 * q + 4, :].bitcast(I32).rearrange("r (z c) -> r z c", z=PASSES),
+                in_=ky_scales[:, 4 * q : 4 * q + 4, :].rearrange("z r c -> r z c").bitcast(I32),
+            )
+
+        def load_words(a):
+            nc.sync.dma_start(out=key_words[a][:].bitcast(I32), in_=ky_words[a].bitcast(I32))
+
+        nc.sync.dma_start(list_b[:], offs2)
+        load_planes(xb_window, xb_planes, "xb", 0, 0, 4)
+        nc.sync.dma_start(out=rows[0:2, :], in_=fk.rearrange("(a k) o -> a (k o)", a=PASSES))
+        nc.sync.dma_start(out=short_rows[0:2, :], in_=tg.rearrange("(h p) o -> h (p o)", h=HALVES))
+        nc.sync.dma_start(out=short_rows[2:4, :], in_=bi.rearrange("o (e p) -> (o e) p", p=P))
+        nc.sync.dma_start(list_k[:], offs3)
+        load_planes(xb_window, xb_planes, "xb", 1, 0, 4)
+        nc.sync.dma_start(list_f[:], offs)
+        for q in range(4):
+            load_scales(q)
+        load_planes(xf_window, xf_planes, "xf", 0, 0, 2)
+        load_planes(xf_window, xf_planes, "xf", 0, 2, 2)
+        for t in range(PACK):
+            load_planes(xf_window, xf_planes, "xf", 1, t, 1)
+        load_words(0)
+        load_words(1)
+
+        identity = keep.tile([P, P], F32, name="identity")
+        make_identity(nc, identity[:])
+
+        factor_ps = psum.tile([P, PACK, P], F32, name="factor_ps")
+        for t in range(PACK):
+            nc.tensor.transpose(factor_ps[:, t, :], rows[:, t : P * PACK : PACK], identity[:])
+        factor = keep.tile([P, PACK, PASSES], F32, name="factor")
+        nc.vector.tensor_copy(out=factor[:], in_=factor_ps[:, :, 0:PASSES])
+        columns_ps = psum.tile([P, P], F32, name="columns_ps")
+        nc.tensor.transpose(columns_ps[:], short_rows[:], identity[:])
+        columns = keep.tile([P, 4], F32, name="columns")
+        nc.vector.tensor_copy(out=columns[:], in_=columns_ps[:, 0:4])
+        bias_ps = psum.tile([P, I], F32, name="bias_ps")
+        for e in range(I // P):
+            nc.tensor.transpose(bias_ps[:, e * P : (e + 1) * P], columns[:, 2 + e : 3 + e].to_broadcast([P, P]), identity[:])
+        threshold = [keep.tile([P, I], F32, name=f"threshold_{h}") for h in range(HALVES)]
+        for h in range(HALVES):
+            nc.vector.tensor_scalar(
+                out=threshold[h][:], in0=bias_ps[:], scalar1=-1.0, scalar2=columns[:, h : h + 1], op0=ALU.mult, op1=ALU.add)
+
+        product = [keep.tile([P, PACK, J], F32, name=f"product_{a}") for a in range(PASSES)]
+        picked_scales = [keep.tile([P, I], U8, name=f"picked_scales_{a}", align_bytes=64) for a in range(PASSES)]
+        scores = [psum.tile([P, I], F32, name=f"scores_{h}") for h in range(HALVES)]
+
+        def gather(on_scalar, picked, window, offsets):
+            if on_scalar:
+                nc.scalar.activation(out=picked, in_=window.indirect(offsets), func=ACT.Copy)
+            else:
+                nc.vector.tensor_copy(out=picked, in_=window.indirect(offsets))
+
+        def multiply(a, t, cols, tokens, entries):
+            nc.vector.scalar_tensor_tensor(
+                out=product[a][:, t, cols], in0=tokens, scalar=factor[:, t, a : a + 1],
+                in1=entries, op0=ALU.mult, op1=ALU.mult)
+
+        def interleave(on_scalar, a, cols):
+            n = cols.stop - cols.start
+            rounded = keep.tile([P, n * PACK], BF16, name=f"rounded_{a}_{cols.start}", align_bytes=64)
+            dst = rounded[:].rearrange("p (c i t) -> p c t i", i=4, t=PACK)
+            src = product[a][:, :, cols].rearrange("p t (c i) -> p c t i", i=4)
+            if on_scalar:
+                nc.scalar.copy(out=dst, in_=src)
+            else:
+                nc.vector.tensor_copy(out=dst, in_=src)
+            return rounded
+
+        def quantize(rounded, a, cols):
+            n = cols.stop - cols.start
+            codes = keep.tile([P, n], U32, name=f"codes_{a}_{cols.start}", align_bytes=64)
+            scales = keep.tile([P, n], U8, name=f"scales_{a}_{cols.start}", align_bytes=64)
+            nc.vector.quantize_mx(out=codes[:].bitcast(E5M2X4), scales=scales[:], in_=rounded[:])
+            return codes, scales
+
+        def product_pass(a, h, codes, scales, words):
+            nc.tensor.matmul_mx(
+                out=scores[h][:], lhsT=codes.bitcast(E5M2X4), lhsT_scale=scales,
+                rhs=words[:].bitcast(E2M1X4), rhs_scale=picked_scales[a][:],
+                start=(a == 0), stop=(a == PASSES - 1))
+
+        whole = slice(0, J)
+        halves = [slice(h * P, (h + 1) * P) for h in range(HALVES)]
+        list_halves = [slice(h * P // 16, (h + 1) * P // 16) for h in range(HALVES)]
+        last = PACK - 1
+
+        for a in range(PASSES):
+            nc.vector.tensor_copy(out=picked_scales[a][:], in_=key_scales[:, a * V : (a + 1) * V].indirect(list_k[:]))
+        entries = {}
+        for a in range(PASSES):
+            for t in range(PACK):
+                if (a, t) != (1, last):
+                    entries[a, t] = keep.tile([P, J], F32, name=f"entries_{a}_{t}", tag=f"plane_{PACK * a + t}", align_bytes=64)
+                    gather(a == 0, entries[a, t][:], xb_window[a, t], list_b[:])
+        last_entries = [keep.tile([P, P], F32, name=f"last_entries_{h}", tag=f"late_{h}", align_bytes=64) for h in range(HALVES)]
+        for h in range(HALVES):
+            gather(False, last_entries[h][:], xb_window[1, last], list_b[:, list_halves[h]])
+        scaled_entries = keep.tile([P, P], F32, name="scaled_entries")
+        nc.vector.tensor_scalar(
+            out=scaled_entries[:], in0=last_entries[0][:], scalar1=factor[:, last, 1:2], scalar2=None, op0=ALU.mult)
+
+        def plane(a, t):
+            n = PACK * a + t
+            if n == PACK * PASSES - 2:
+                tokens = product[1][:, last, :]
+            else:
+                tile = keep.tile([P, J], F32, name=f"tokens_{n}", tag=f"plane_{n - 2}", align_bytes=64)
+                tokens = tile[:]
+            gather(True, tokens, xf_window[a, t], list_f[:])
+            multiply(a, t, whole, tokens, entries[a, t][:])
+
+        for t in range(PACK):
+            plane(0, t)
+        rounded = interleave(False, 0, whole)
+        first_codes, first_scales = quantize(rounded, 0, whole)
+
+        for t in range(last):
+            plane(1, t)
+        nc.vector.tensor_tensor(
+            out=product[1][:, last, halves[0]], in0=xf_window[1, last].indirect(list_f[:, list_halves[0]]),
+            in1=scaled_entries[:], op=ALU.mult)
+        last_tokens = keep.tile([P, P], F32, name="last_tokens", tag="plane_5", align_bytes=64)
+        gather(True, last_tokens[:], xf_window[1, last], list_f[:, list_halves[1]])
+        multiply(1, last, halves[1], last_tokens[:], last_entries[1][:])
+        rounded = [interleave(True, 1, halves[h]) for h in range(HALVES)]
+        picked_words = [keep.tile([P, I], U16, name=f"picked_words_{a}", tag=("plane_5", "late_1")[a], align_bytes=64) for a in range(PASSES)]
+        nc.vector.tensor_copy(out=picked_words[0][:], in_=key_words[0][:].indirect(list_k[:]))
+        for h in range(HALVES):
+            product_pass(0, h, first_codes[:, halves[h]], first_scales[:, halves[h]], picked_words[0])
+        nc.vector.tensor_copy(out=picked_words[1][:], in_=key_words[1][:].indirect(list_k[:]))
+        for h in range(HALVES):
+            codes, scales = quantize(rounded[h], 1, halves[h])
+            product_pass(1, h, codes[:], scales[:], picked_words[1])
+
+        excess = [keep.tile([P, I], F32, name=f"excess_{h}") for h in range(HALVES)]
+        result = [keep.tile([P, I], F32, name=f"result_{h}") for h in range(HALVES)]
+        for h in range(HALVES):
+            nc.vector.tensor_tensor(out=excess[h][:], in0=scores[h][:], in1=threshold[h][:], op=ALU.subtract)
+        for h in range(HALVES):
+            nc.vector.scalar_tensor_tensor(
+                out=result[h][:], in0=excess[h][:], scalar=0.0, in1=excess[h][:], op0=ALU.max, op1=ALU.mult)
+            nc.sync.dma_start(out=out[halves[h], :], in_=result[h][:])

@@ -39,7 +39,7 @@ def tile_list_scores_products_listed_hinge_kernel(tc, xf, xb, fk, ky_words, ky_s
 
         def load_planes(windows, planes, label, a, first, count):
             width = planes.shape[3]
-            tile = keep.tile([P, count * width], F32, name=f"{label}_{a}_{first}")
+            tile = keep.tile([P, count * width], F32, name=f"{label}_{a}_{first}", align_bytes=64)
             nc.sync.dma_start(out=tile[:], in_=planes[a][:, first : first + count, :].rearrange("p t w -> p (t w)"))
             for t in range(count):
                 windows[a, first + t] = tile[:, t * width : (t + 1) * width]
@@ -63,16 +63,17 @@ def tile_list_scores_products_listed_hinge_kernel(tc, xf, xb, fk, ky_words, ky_s
 
         nc.sync.dma_start(list_b[:], offs2)
         load_planes(xb_window, xb_planes, "xb", 0, 0, 4)
-        nc.sync.dma_start(out=rows[0:2, :], in_=fk.rearrange("(a k) o -> a (k o)", a=PASSES))
-        nc.sync.dma_start(out=short_rows[0:2, :], in_=tg.rearrange("(h p) o -> h (p o)", h=HALVES))
-        nc.sync.dma_start(out=short_rows[2:4, :], in_=bi.rearrange("o (e p) -> (o e) p", p=P))
+        nc.sync.dma_start(out=rows[8:10, :], in_=fk.rearrange("(a k) o -> a (k o)", a=PASSES))
+        nc.sync.dma_start(out=short_rows[16:18, :], in_=tg.rearrange("(h p) o -> h (p o)", h=HALVES))
+        nc.sync.dma_start(out=short_rows[20:22, :], in_=bi.rearrange("o (e p) -> (o e) p", p=P))
         nc.sync.dma_start(list_k[:], offs3)
         load_planes(xb_window, xb_planes, "xb", 1, 0, 4)
         nc.sync.dma_start(list_f[:], offs)
         for q in range(4):
             load_scales(q)
         load_planes(xf_window, xf_planes, "xf", 0, 0, 2)
-        load_planes(xf_window, xf_planes, "xf", 0, 2, 2)
+        load_planes(xf_window, xf_planes, "xf", 0, 2, 1)
+        load_planes(xf_window, xf_planes, "xf", 0, 3, 1)
         for t in range(PACK):
             load_planes(xf_window, xf_planes, "xf", 1, t, 1)
         load_words(0)
@@ -85,20 +86,21 @@ def tile_list_scores_products_listed_hinge_kernel(tc, xf, xb, fk, ky_words, ky_s
         for t in range(PACK):
             nc.tensor.transpose(factor_ps[:, t, :], rows[:, t : P * PACK : PACK], identity[:])
         factor = keep.tile([P, PACK, PASSES], F32, name="factor")
-        nc.vector.tensor_copy(out=factor[:], in_=factor_ps[:, :, 0:PASSES])
+        nc.vector.tensor_copy(out=factor[:], in_=factor_ps[:, :, 8:10])
         columns_ps = psum.tile([P, P], F32, name="columns_ps")
         nc.tensor.transpose(columns_ps[:], short_rows[:], identity[:])
-        columns = keep.tile([P, 4], F32, name="columns")
-        nc.vector.tensor_copy(out=columns[:], in_=columns_ps[:, 0:4])
+        columns = keep.tile([P, 6], F32, name="columns")
+        nc.vector.tensor_copy(out=columns[:], in_=columns_ps[:, 16:22])
         bias_ps = psum.tile([P, I], F32, name="bias_ps")
         for e in range(I // P):
-            nc.tensor.transpose(bias_ps[:, e * P : (e + 1) * P], columns[:, 2 + e : 3 + e].to_broadcast([P, P]), identity[:])
+            nc.tensor.transpose(bias_ps[:, e * P : (e + 1) * P], columns[:, 4 + e : 5 + e].to_broadcast([P, P]), identity[:])
         threshold = [keep.tile([P, I], F32, name=f"threshold_{h}") for h in range(HALVES)]
         for h in range(HALVES):
             nc.vector.tensor_scalar(
                 out=threshold[h][:], in0=bias_ps[:], scalar1=-1.0, scalar2=columns[:, h : h + 1], op0=ALU.mult, op1=ALU.add)
 
-        product = [keep.tile([P, PACK, J], F32, name=f"product_{a}") for a in range(PASSES)]
+        product_tiles = [keep.tile([P, PACK * J], F32, name=f"product_{a}", align_bytes=64) for a in range(PASSES)]
+        product = [tile[:].rearrange("p (t c) -> p t c", t=PACK) for tile in product_tiles]
         picked_scales = [keep.tile([P, I], U8, name=f"picked_scales_{a}", align_bytes=64) for a in range(PASSES)]
         scores = [psum.tile([P, I], F32, name=f"scores_{h}") for h in range(HALVES)]
 
@@ -113,22 +115,19 @@ def tile_list_scores_products_listed_hinge_kernel(tc, xf, xb, fk, ky_words, ky_s
                 out=product[a][:, t, cols], in0=tokens, scalar=factor[:, t, a : a + 1],
                 in1=entries, op0=ALU.mult, op1=ALU.mult)
 
-        def interleave(on_scalar, a, cols):
-            n = cols.stop - cols.start
-            rounded = keep.tile([P, n * PACK], BF16, name=f"rounded_{a}_{cols.start}", align_bytes=64)
-            dst = rounded[:].rearrange("p (c i t) -> p c t i", i=4, t=PACK)
+        def interleave(on_scalar, a, cols, rounded):
+            dst = rounded.rearrange("p (c i t) -> p c t i", i=4, t=PACK)
             src = product[a][:, :, cols].rearrange("p t (c i) -> p c t i", i=4)
             if on_scalar:
                 nc.scalar.copy(out=dst, in_=src)
             else:
                 nc.vector.tensor_copy(out=dst, in_=src)
-            return rounded
 
-        def quantize(rounded, a, cols):
+        def quantize(rounded, a, cols, tag):
             n = cols.stop - cols.start
-            codes = keep.tile([P, n], U32, name=f"codes_{a}_{cols.start}", align_bytes=64)
+            codes = keep.tile([P, n], U32, name=f"codes_{a}_{cols.start}", tag=tag, align_bytes=64)
             scales = keep.tile([P, n], U8, name=f"scales_{a}_{cols.start}", align_bytes=64)
-            nc.vector.quantize_mx(out=codes[:].bitcast(E5M2X4), scales=scales[:], in_=rounded[:])
+            nc.vector.quantize_mx(out=codes[:].bitcast(E5M2X4), scales=scales[:], in_=rounded)
             return codes, scales
 
         def product_pass(a, h, codes, scales, words):
@@ -145,49 +144,55 @@ def tile_list_scores_products_listed_hinge_kernel(tc, xf, xb, fk, ky_words, ky_s
         for a in range(PASSES):
             nc.vector.tensor_copy(out=picked_scales[a][:], in_=key_scales[:, a * V : (a + 1) * V].indirect(list_k[:]))
         entries = {}
+        borrowed = {(0, 3): 0, (1, 0): 2, (1, 1): 3}
         for a in range(PASSES):
             for t in range(PACK):
-                if (a, t) != (1, last):
-                    entries[a, t] = keep.tile([P, J], F32, name=f"entries_{a}_{t}", tag=f"plane_{PACK * a + t}", align_bytes=64)
-                    gather(a == 0, entries[a, t][:], xb_window[a, t], list_b[:])
-        last_entries = [keep.tile([P, P], F32, name=f"last_entries_{h}", tag=f"late_{h}", align_bytes=64) for h in range(HALVES)]
+                if (a, t) in borrowed:
+                    entries[a, t] = product[1][:, borrowed[a, t], :]
+                else:
+                    tile = keep.tile([P, J], F32, name=f"entries_{a}_{t}", align_bytes=64)
+                    entries[a, t] = tile[:]
+                gather(a == 0 or t == 0, entries[a, t], xb_window[a, t], list_b[:])
+        last_scaled = keep.tile([P, J], F32, name="last_scaled", align_bytes=64)
+        third_scaled = keep.tile([P, J], F32, name="third_scaled", align_bytes=64)
+        scaled = {2: third_scaled[:], 3: last_scaled[:]}
+        for t in (2, 3):
+            nc.vector.tensor_scalar(
+                out=scaled[t], in0=entries[1, t], scalar1=factor[:, t, 1:2], scalar2=None, op0=ALU.mult)
+
+        def plane(a, t, tag):
+            tokens = keep.tile([P, J], F32, name=f"tokens_{a}_{t}", tag=tag, align_bytes=64)
+            gather(True, tokens[:], xf_window[a, t], list_f[:])
+            multiply(a, t, whole, tokens[:], entries[a, t])
+
+        def fused(t, cols, list_cols):
+            nc.vector.tensor_tensor(
+                out=product[1][:, t, cols], in0=xf_window[1, t].indirect(list_f[:, list_cols]), in1=scaled[t][:, cols], op=ALU.mult)
+
+        plane(0, 0, "tokens_0_0")
+        plane(0, 1, "tokens_0_1")
+        plane(0, 2, "entries_0_0")
+        plane(0, 3, "entries_0_1")
+        first_rounded_tile = keep.tile([P, J * PACK], BF16, name="first_rounded", align_bytes=64)
+        first_rounded = first_rounded_tile[:]
+        interleave(False, 0, whole, first_rounded)
+        first_codes, first_scales = quantize(first_rounded, 0, whole, "first_codes")
+
+        plane(1, 0, "entries_0_2")
+        plane(1, 1, "entries_0_1")
+        fused(2, whole, slice(0, J // 16))
         for h in range(HALVES):
-            gather(False, last_entries[h][:], xb_window[1, last], list_b[:, list_halves[h]])
-        scaled_entries = keep.tile([P, P], F32, name="scaled_entries")
-        nc.vector.tensor_scalar(
-            out=scaled_entries[:], in0=last_entries[0][:], scalar1=factor[:, last, 1:2], scalar2=None, op0=ALU.mult)
-
-        def plane(a, t):
-            n = PACK * a + t
-            if n == PACK * PASSES - 2:
-                tokens = product[1][:, last, :]
-            else:
-                tile = keep.tile([P, J], F32, name=f"tokens_{n}", tag=f"plane_{n - 2}", align_bytes=64)
-                tokens = tile[:]
-            gather(True, tokens, xf_window[a, t], list_f[:])
-            multiply(a, t, whole, tokens, entries[a, t][:])
-
-        for t in range(PACK):
-            plane(0, t)
-        rounded = interleave(False, 0, whole)
-        first_codes, first_scales = quantize(rounded, 0, whole)
-
-        for t in range(last):
-            plane(1, t)
-        nc.vector.tensor_tensor(
-            out=product[1][:, last, halves[0]], in0=xf_window[1, last].indirect(list_f[:, list_halves[0]]),
-            in1=scaled_entries[:], op=ALU.mult)
-        last_tokens = keep.tile([P, P], F32, name="last_tokens", tag="plane_5", align_bytes=64)
-        gather(True, last_tokens[:], xf_window[1, last], list_f[:, list_halves[1]])
-        multiply(1, last, halves[1], last_tokens[:], last_entries[1][:])
-        rounded = [interleave(True, 1, halves[h]) for h in range(HALVES)]
-        picked_words = [keep.tile([P, I], U16, name=f"picked_words_{a}", tag=("plane_5", "late_1")[a], align_bytes=64) for a in range(PASSES)]
+            fused(last, halves[h], list_halves[h])
+        rounded = [keep.tile([P, P * PACK], BF16, name=f"rounded_{h}", align_bytes=64) for h in range(HALVES)]
+        for h in range(HALVES):
+            interleave(True, 1, halves[h], rounded[h][:])
+        picked_words = [keep.tile([P, I], U16, name=f"picked_words_{a}", tag=("last_scaled", "xf_1_3")[a], align_bytes=64) for a in range(PASSES)]
         nc.vector.tensor_copy(out=picked_words[0][:], in_=key_words[0][:].indirect(list_k[:]))
         for h in range(HALVES):
             product_pass(0, h, first_codes[:, halves[h]], first_scales[:, halves[h]], picked_words[0])
         nc.vector.tensor_copy(out=picked_words[1][:], in_=key_words[1][:].indirect(list_k[:]))
         for h in range(HALVES):
-            codes, scales = quantize(rounded[h], 1, halves[h])
+            codes, scales = quantize(rounded[h][:], 1, halves[h], ("second_codes", "key_words_1")[h])
             product_pass(1, h, codes[:], scales[:], picked_words[1])
 
         excess = [keep.tile([P, I], F32, name=f"excess_{h}") for h in range(HALVES)]

@@ -21,6 +21,12 @@ P = 128
 PACK = 4
 PASSES = K // (P * PACK)
 HALVES = J // P
+QUADRANTS = 4
+ENTRIES_A_COLUMN = 16
+RUN = 4
+FK_ROW = 8
+BI_ROW = 20
+TARGET_PITCH = 8
 
 
 def tile_list_scores_products_listed_hinge_kernel(tc, xf, xb, fk, ky_words, ky_scales, bi, tg, offs, offs2, offs3, out):
@@ -29,9 +35,9 @@ def tile_list_scores_products_listed_hinge_kernel(tc, xf, xb, fk, ky_words, ky_s
         keep = ctx.enter_context(tc.tile_pool(name="keep", bufs=1))
         psum = ctx.enter_context(tc.psum_pool(name="psum", bufs=1))
 
-        list_f = keep.tile([P, J // 16], U16, name="list_f")
-        list_b = keep.tile([P, J // 16], U16, name="list_b")
-        list_k = keep.tile([P, I // 16], U16, name="list_k")
+        list_f = keep.tile([P, J // ENTRIES_A_COLUMN], U16, name="list_f")
+        list_b = keep.tile([P, J // ENTRIES_A_COLUMN], U16, name="list_b")
+        list_k = keep.tile([P, I // ENTRIES_A_COLUMN], U16, name="list_k")
 
         xf_planes = xf.rearrange("(a p t) w -> a p t w", a=PASSES, t=PACK)
         xb_planes = xb.rearrange("(a p t) w -> a p t w", a=PASSES, t=PACK)
@@ -44,90 +50,113 @@ def tile_list_scores_products_listed_hinge_kernel(tc, xf, xb, fk, ky_words, ky_s
             for t in range(count):
                 windows[a, first + t] = tile[:, t * width : (t + 1) * width]
 
-        rows = keep.tile([P, P * PACK], F32, name="rows")
-        nc.vector.memset(rows[:], 0.0)
-        short_rows = keep.tile([P, P], F32, name="short_rows")
-        nc.vector.memset(short_rows[:], 0.0)
+        fk_rows = keep.tile([P, P * PACK], F32, name="fk_rows")
+        nc.vector.memset(fk_rows[:], 0.0)
+        bi_rows = keep.tile([P, P], F32, name="bi_rows")
+        nc.vector.memset(bi_rows[:], 0.0)
         key_scales = keep.tile([P, PASSES * V], U8, name="key_scales", align_bytes=64)
         nc.vector.memset(key_scales[:].bitcast(I32), 0)
         key_words = [keep.tile([P, V], U16, name=f"key_words_{a}", align_bytes=64) for a in range(PASSES)]
 
-        def load_scales(q):
-            nc.sync.dma_start(
-                out=key_scales[32 * q : 32 * q + 4, :].bitcast(I32).rearrange("r (z c) -> r z c", z=PASSES),
-                in_=ky_scales[:, 4 * q : 4 * q + 4, :].rearrange("z r c -> r z c").bitcast(I32),
-            )
-
-        def load_words(a):
-            nc.sync.dma_start(out=key_words[a][:].bitcast(I32), in_=ky_words[a].bitcast(I32))
-
+        load_planes(xb_window, xb_planes, "xb", 0, 0, PACK)
         nc.sync.dma_start(list_b[:], offs2)
-        load_planes(xb_window, xb_planes, "xb", 0, 0, 4)
-        nc.sync.dma_start(out=rows[8:10, :], in_=fk.rearrange("(a k) o -> a (k o)", a=PASSES))
-        nc.sync.dma_start(out=short_rows[16:18, :], in_=tg.rearrange("(h p) o -> h (p o)", h=HALVES))
-        nc.sync.dma_start(out=short_rows[20:22, :], in_=bi.rearrange("o (e p) -> (o e) p", p=P))
+        nc.sync.dma_start(out=fk_rows[FK_ROW : FK_ROW + PASSES, :], in_=fk.rearrange("(a k) o -> a (k o)", a=PASSES))
+        nc.sync.dma_start(out=bi_rows[BI_ROW : BI_ROW + I // P, :], in_=bi.rearrange("o (e p) -> (o e) p", p=P))
         nc.sync.dma_start(list_k[:], offs3)
-        load_planes(xb_window, xb_planes, "xb", 1, 0, 4)
+        load_planes(xb_window, xb_planes, "xb", 1, 0, PACK)
         nc.sync.dma_start(list_f[:], offs)
-        for q in range(4):
-            load_scales(q)
-        load_planes(xf_window, xf_planes, "xf", 0, 0, 2)
-        load_planes(xf_window, xf_planes, "xf", 0, 2, 1)
-        load_planes(xf_window, xf_planes, "xf", 0, 3, 1)
+        for q in range(QUADRANTS):
+            nc.sync.dma_start(
+                out=key_scales[32 * q : 32 * q + 4, :].bitcast(I32).rearrange("r (a c) -> r a c", a=PASSES),
+                in_=ky_scales[:, 4 * q : 4 * q + 4, :].rearrange("a r c -> r a c").bitcast(I32),
+            )
+        for t in range(0, PACK, 2):
+            load_planes(xf_window, xf_planes, "xf", 0, t, 2)
         for t in range(PACK):
             load_planes(xf_window, xf_planes, "xf", 1, t, 1)
-        load_words(0)
-        load_words(1)
+        for a in range(PASSES):
+            nc.sync.dma_start(out=key_words[a][:].bitcast(I32), in_=ky_words[a].bitcast(I32))
+        target = keep.tile([P, HALVES, TARGET_PITCH], F32, name="target")
+        with nc.allow_non_contiguous_dma(reason="one target a partition and half"):
+            nc.sync.dma_start(out=target[:, :, 0:1], in_=tg.rearrange("(h p) o -> p h o", h=HALVES))
 
         identity = keep.tile([P, P], F32, name="identity")
         make_identity(nc, identity[:])
 
         factor_ps = psum.tile([P, PACK, P], F32, name="factor_ps")
         for t in range(PACK):
-            nc.tensor.transpose(factor_ps[:, t, :], rows[:, t : P * PACK : PACK], identity[:])
+            nc.tensor.transpose(factor_ps[:, t, :], fk_rows[:, t : P * PACK : PACK], identity[:])
         factor = keep.tile([P, PACK, PASSES], F32, name="factor")
-        nc.vector.tensor_copy(out=factor[:], in_=factor_ps[:, :, 8:10])
-        columns_ps = psum.tile([P, P], F32, name="columns_ps")
-        nc.tensor.transpose(columns_ps[:], short_rows[:], identity[:])
-        columns = keep.tile([P, 6], F32, name="columns")
-        nc.vector.tensor_copy(out=columns[:], in_=columns_ps[:, 16:22])
+        nc.vector.tensor_copy(out=factor[:], in_=factor_ps[:, :, FK_ROW : FK_ROW + PASSES])
+        bi_columns_ps = psum.tile([P, P], F32, name="bi_columns_ps")
+        nc.tensor.transpose(bi_columns_ps[:], bi_rows[:], identity[:])
+        bi_columns = keep.tile([P, I // P], F32, name="bi_columns")
+        nc.vector.tensor_copy(out=bi_columns[:], in_=bi_columns_ps[:, BI_ROW : BI_ROW + I // P])
         bias_ps = psum.tile([P, I], F32, name="bias_ps")
         for e in range(I // P):
-            nc.tensor.transpose(bias_ps[:, e * P : (e + 1) * P], columns[:, 4 + e : 5 + e].to_broadcast([P, P]), identity[:])
-        threshold = [keep.tile([P, I], F32, name=f"threshold_{h}") for h in range(HALVES)]
-        for h in range(HALVES):
-            nc.vector.tensor_scalar(
-                out=threshold[h][:], in0=bias_ps[:], scalar1=-1.0, scalar2=columns[:, h : h + 1], op0=ALU.mult, op1=ALU.add)
+            nc.tensor.transpose(
+                bias_ps[:, e * P : (e + 1) * P], bi_columns[:, e : e + 1].to_broadcast([P, P]), identity[:])
+        bias = keep.tile([P, I], F32, name="bias")
+        nc.vector.tensor_copy(out=bias[:], in_=bias_ps[:])
 
         product_tiles = [keep.tile([P, PACK * J], F32, name=f"product_{a}", align_bytes=64) for a in range(PASSES)]
         product = [tile[:].rearrange("p (t c) -> p t c", t=PACK) for tile in product_tiles]
         picked_scales = [keep.tile([P, I], U8, name=f"picked_scales_{a}", align_bytes=64) for a in range(PASSES)]
         scores = [psum.tile([P, I], F32, name=f"scores_{h}") for h in range(HALVES)]
 
-        def gather(on_scalar, picked, window, offsets):
-            if on_scalar:
-                nc.scalar.activation(out=picked, in_=window.indirect(offsets), func=ACT.Copy)
-            else:
-                nc.vector.tensor_copy(out=picked, in_=window.indirect(offsets))
+        whole = slice(0, J)
+        halves = [slice(h * P, (h + 1) * P) for h in range(HALVES)]
+        list_halves = [slice(h * P // ENTRIES_A_COLUMN, (h + 1) * P // ENTRIES_A_COLUMN) for h in range(HALVES)]
+        third, last = PACK - 2, PACK - 1
 
-        def multiply(a, t, cols, tokens, entries):
+        for a in range(PASSES):
+            nc.vector.tensor_copy(out=picked_scales[a][:], in_=key_scales[:, a * V : (a + 1) * V].indirect(list_k[:]))
+
+        entries = {}
+        borrowed_plane = {(0, last): 0, (1, 0): third, (1, 1): last}
+        for a in range(PASSES):
+            for t in range(PACK):
+                if (a, t) in borrowed_plane:
+                    entries[a, t] = product[1][:, borrowed_plane[a, t], :]
+                else:
+                    tile = keep.tile([P, J], F32, name=f"entries_{a}_{t}", align_bytes=64)
+                    entries[a, t] = tile[:]
+                looked_up = xb_window[a, t].indirect(list_b[:])
+                if a == 0 or t == 0:
+                    nc.scalar.activation(out=entries[a, t], in_=looked_up, func=ACT.Copy)
+                else:
+                    nc.vector.tensor_copy(out=entries[a, t], in_=looked_up)
+
+        last_scaled = [keep.tile([P, P], F32, name=f"last_scaled_{h}", align_bytes=64) for h in range(HALVES)]
+        third_scaled = keep.tile([P, J], F32, name="third_scaled", align_bytes=64)
+        nc.vector.tensor_scalar(
+            out=third_scaled[:], in0=entries[1, third], scalar1=factor[:, third, 1:2], scalar2=None, op0=ALU.mult)
+        for h in range(HALVES):
+            nc.vector.tensor_scalar(
+                out=last_scaled[h][:], in0=entries[1, last][:, halves[h]], scalar1=factor[:, last, 1:2], scalar2=None,
+                op0=ALU.mult)
+
+        def multiply_plane(a, t, tag):
+            tokens = keep.tile([P, J], F32, name=f"tokens_{a}_{t}", tag=tag, align_bytes=64)
+            nc.scalar.activation(out=tokens[:], in_=xf_window[a, t].indirect(list_f[:]), func=ACT.Copy)
             nc.vector.scalar_tensor_tensor(
-                out=product[a][:, t, cols], in0=tokens, scalar=factor[:, t, a : a + 1],
-                in1=entries, op0=ALU.mult, op1=ALU.mult)
+                out=product[a][:, t, :], in0=tokens[:], scalar=factor[:, t, a : a + 1], in1=entries[a, t],
+                op0=ALU.mult, op1=ALU.mult)
 
-        def interleave(on_scalar, a, cols, rounded):
-            dst = rounded.rearrange("p (c i t) -> p c t i", i=4, t=PACK)
-            src = product[a][:, :, cols].rearrange("p t (c i) -> p c t i", i=4)
-            if on_scalar:
-                nc.scalar.copy(out=dst, in_=src)
-            else:
-                nc.vector.tensor_copy(out=dst, in_=src)
+        def multiply_fused(t, cols, offsets, scaled):
+            nc.vector.tensor_tensor(
+                out=product[1][:, t, cols], in0=xf_window[1, t].indirect(offsets), in1=scaled, op=ALU.mult)
 
-        def quantize(rounded, a, cols, tag):
-            n = cols.stop - cols.start
-            codes = keep.tile([P, n], U32, name=f"codes_{a}_{cols.start}", tag=tag, align_bytes=64)
-            scales = keep.tile([P, n], U8, name=f"scales_{a}_{cols.start}", align_bytes=64)
-            nc.vector.quantize_mx(out=codes[:].bitcast(E5M2X4), scales=scales[:], in_=rounded)
+        def interleave(copy, a, cols, rounded):
+            copy(
+                out=rounded[:].rearrange("p (c i t) -> p c t i", i=RUN, t=PACK),
+                in_=product[a][:, :, cols].rearrange("p t (c i) -> p c t i", i=RUN))
+
+        def quantize(rounded, label):
+            width = rounded.shape[1] // PACK
+            codes = keep.tile([P, width], U32, name=f"codes_{label}", align_bytes=64)
+            scales = keep.tile([P, width], U8, name=f"scales_{label}", align_bytes=64)
+            nc.vector.quantize_mx(out=codes[:].bitcast(E5M2X4), scales=scales[:], in_=rounded[:])
             return codes, scales
 
         def product_pass(a, h, codes, scales, words):
@@ -136,69 +165,40 @@ def tile_list_scores_products_listed_hinge_kernel(tc, xf, xb, fk, ky_words, ky_s
                 rhs=words[:].bitcast(E2M1X4), rhs_scale=picked_scales[a][:],
                 start=(a == 0), stop=(a == PASSES - 1))
 
-        whole = slice(0, J)
-        halves = [slice(h * P, (h + 1) * P) for h in range(HALVES)]
-        list_halves = [slice(h * P // 16, (h + 1) * P // 16) for h in range(HALVES)]
-        last = PACK - 1
+        multiply_plane(0, 0, "tokens_0_0")
+        multiply_plane(0, 1, "tokens_0_1")
+        multiply_plane(0, 2, "entries_0_0")
+        multiply_plane(0, 3, "entries_0_1")
+        first_rounded = keep.tile([P, J * PACK], BF16, name="first_rounded", align_bytes=64)
+        interleave(nc.vector.tensor_copy, 0, whole, first_rounded)
+        first_codes, first_scales = quantize(first_rounded, "first")
 
-        for a in range(PASSES):
-            nc.vector.tensor_copy(out=picked_scales[a][:], in_=key_scales[:, a * V : (a + 1) * V].indirect(list_k[:]))
-        entries = {}
-        borrowed = {(0, 3): 0, (1, 0): 2, (1, 1): 3}
-        for a in range(PASSES):
-            for t in range(PACK):
-                if (a, t) in borrowed:
-                    entries[a, t] = product[1][:, borrowed[a, t], :]
-                else:
-                    tile = keep.tile([P, J], F32, name=f"entries_{a}_{t}", align_bytes=64)
-                    entries[a, t] = tile[:]
-                gather(a == 0 or t == 0, entries[a, t], xb_window[a, t], list_b[:])
-        last_scaled = keep.tile([P, J], F32, name="last_scaled", align_bytes=64)
-        third_scaled = keep.tile([P, J], F32, name="third_scaled", align_bytes=64)
-        scaled = {2: third_scaled[:], 3: last_scaled[:]}
-        for t in (2, 3):
-            nc.vector.tensor_scalar(
-                out=scaled[t], in0=entries[1, t], scalar1=factor[:, t, 1:2], scalar2=None, op0=ALU.mult)
-
-        def plane(a, t, tag):
-            tokens = keep.tile([P, J], F32, name=f"tokens_{a}_{t}", tag=tag, align_bytes=64)
-            gather(True, tokens[:], xf_window[a, t], list_f[:])
-            multiply(a, t, whole, tokens[:], entries[a, t])
-
-        def fused(t, cols, list_cols):
-            nc.vector.tensor_tensor(
-                out=product[1][:, t, cols], in0=xf_window[1, t].indirect(list_f[:, list_cols]), in1=scaled[t][:, cols], op=ALU.mult)
-
-        plane(0, 0, "tokens_0_0")
-        plane(0, 1, "tokens_0_1")
-        plane(0, 2, "entries_0_0")
-        plane(0, 3, "entries_0_1")
-        first_rounded_tile = keep.tile([P, J * PACK], BF16, name="first_rounded", align_bytes=64)
-        first_rounded = first_rounded_tile[:]
-        interleave(False, 0, whole, first_rounded)
-        first_codes, first_scales = quantize(first_rounded, 0, whole, "first_codes")
-
-        plane(1, 0, "entries_0_2")
-        plane(1, 1, "entries_0_1")
-        fused(2, whole, slice(0, J // 16))
+        multiply_plane(1, 0, "entries_0_2")
+        multiply_plane(1, 1, "entries_0_1")
+        multiply_fused(third, whole, list_f[:], third_scaled[:])
         for h in range(HALVES):
-            fused(last, halves[h], list_halves[h])
-        rounded = [keep.tile([P, P * PACK], BF16, name=f"rounded_{h}", align_bytes=64) for h in range(HALVES)]
-        for h in range(HALVES):
-            interleave(True, 1, halves[h], rounded[h][:])
-        picked_words = [keep.tile([P, I], U16, name=f"picked_words_{a}", tag=("last_scaled", "xf_1_3")[a], align_bytes=64) for a in range(PASSES)]
+            multiply_fused(last, halves[h], list_f[:, list_halves[h]], last_scaled[h][:])
+        rounded_0 = keep.tile([P, P * PACK], BF16, name="rounded_0", align_bytes=64)
+        interleave(nc.scalar.copy, 1, halves[0], rounded_0)
+        picked_words = [
+            keep.tile([P, I], U16, name=f"picked_words_{a}", tag=f"last_scaled_{a}", align_bytes=64)
+            for a in range(PASSES)]
         nc.vector.tensor_copy(out=picked_words[0][:], in_=key_words[0][:].indirect(list_k[:]))
+        rounded_1 = keep.tile([P, P * PACK], BF16, name="rounded_1", tag="key_words_0", align_bytes=64)
+        interleave(nc.scalar.copy, 1, halves[1], rounded_1)
         for h in range(HALVES):
             product_pass(0, h, first_codes[:, halves[h]], first_scales[:, halves[h]], picked_words[0])
         nc.vector.tensor_copy(out=picked_words[1][:], in_=key_words[1][:].indirect(list_k[:]))
-        for h in range(HALVES):
-            codes, scales = quantize(rounded[h][:], 1, halves[h], ("second_codes", "key_words_1")[h])
+        for h, rounded in enumerate((rounded_0, rounded_1)):
+            codes, scales = quantize(rounded, f"second_{h}")
             product_pass(1, h, codes[:], scales[:], picked_words[1])
 
         excess = [keep.tile([P, I], F32, name=f"excess_{h}") for h in range(HALVES)]
         result = [keep.tile([P, I], F32, name=f"result_{h}") for h in range(HALVES)]
         for h in range(HALVES):
-            nc.vector.tensor_tensor(out=excess[h][:], in0=scores[h][:], in1=threshold[h][:], op=ALU.subtract)
+            nc.vector.scalar_tensor_tensor(
+                out=excess[h][:], in0=scores[h][:], scalar=target[:, h, 0:1], in1=bias[:],
+                op0=ALU.subtract, op1=ALU.add)
         for h in range(HALVES):
             nc.vector.scalar_tensor_tensor(
                 out=result[h][:], in0=excess[h][:], scalar=0.0, in1=excess[h][:], op0=ALU.max, op1=ALU.mult)

from contextlib import ExitStack

import concourse.mybir as mybir
from concourse.masks import make_identity

K, T, J, I, S, V = 1024, 1024, 256, 256, 512, 1024
FLOPS = 2 * K * J * I

F32 = mybir.dt.float32
BF16 = mybir.dt.bfloat16
I32 = mybir.dt.int32
U32 = mybir.dt.uint32
U16 = mybir.dt.uint16
U8 = mybir.dt.uint8
E5M2X4 = mybir.dt.float8_e5m2_x4
E2M1X4 = mybir.dt.float4_e2m1fn_x4
ALU = mybir.AluOpType
ACT = mybir.ActivationFunctionType

P = 128
PACK = 4
PASSES = K // (P * PACK)
HALVES = J // P
QUADRANTS = 4
ENTRIES_A_COLUMN = 16
RUN = 4
FK_ROW = 8
BI_ROW = 20
TARGET_PITCH = 8


def tile_list_scores_products_listed_hinge_kernel(tc, xf, xb, fk, ky_words, ky_scales, bi, tg, offs, offs2, offs3, out):
    nc = tc.nc
    with ExitStack() as ctx:
        keep = ctx.enter_context(tc.tile_pool(name="keep", bufs=1))
        psum = ctx.enter_context(tc.psum_pool(name="psum", bufs=1))

        list_f = keep.tile([P, J // ENTRIES_A_COLUMN], U16, name="list_f")
        list_b = keep.tile([P, J // ENTRIES_A_COLUMN], U16, name="list_b")
        list_k = keep.tile([P, I // ENTRIES_A_COLUMN], U16, name="list_k")

        xf_planes = xf.rearrange("(a p t) w -> a p t w", a=PASSES, t=PACK)
        xb_planes = xb.rearrange("(a p t) w -> a p t w", a=PASSES, t=PACK)
        xf_window, xb_window = {}, {}

        def load_planes(windows, planes, label, a, first, count):
            width = planes.shape[3]
            tile = keep.tile([P, count * width], F32, name=f"{label}_{a}_{first}", align_bytes=64)
            nc.sync.dma_start(out=tile[:], in_=planes[a][:, first : first + count, :].rearrange("p t w -> p (t w)"))
            for t in range(count):
                windows[a, first + t] = tile[:, t * width : (t + 1) * width]

        fk_rows = keep.tile([P, P * PACK], F32, name="fk_rows")
        nc.vector.memset(fk_rows[:], 0.0)
        bi_rows = keep.tile([P, P], F32, name="bi_rows")
        nc.vector.memset(bi_rows[:], 0.0)
        key_scales = keep.tile([P, PASSES * V], U8, name="key_scales", align_bytes=64)
        nc.vector.memset(key_scales[:].bitcast(I32), 0)
        key_words = [keep.tile([P, V], U16, name=f"key_words_{a}", align_bytes=64) for a in range(PASSES)]

        load_planes(xb_window, xb_planes, "xb", 0, 0, PACK)
        nc.sync.dma_start(list_b[:], offs2)
        nc.sync.dma_start(out=fk_rows[FK_ROW : FK_ROW + PASSES, :], in_=fk.rearrange("(a k) o -> a (k o)", a=PASSES))
        nc.sync.dma_start(out=bi_rows[BI_ROW : BI_ROW + I // P, :], in_=bi.rearrange("o (e p) -> (o e) p", p=P))
        nc.sync.dma_start(list_k[:], offs3)
        load_planes(xb_window, xb_planes, "xb", 1, 0, PACK)
        nc.sync.dma_start(list_f[:], offs)
        for q in range(QUADRANTS):
            nc.sync.dma_start(
                out=key_scales[32 * q : 32 * q + 4, :].bitcast(I32).rearrange("r (a c) -> r a c", a=PASSES),
                in_=ky_scales[:, 4 * q : 4 * q + 4, :].rearrange("a r c -> r a c").bitcast(I32),
            )
        for t in range(0, PACK, 2):
            load_planes(xf_window, xf_planes, "xf", 0, t, 2)
        for t in range(PACK):
            load_planes(xf_window, xf_planes, "xf", 1, t, 1)
        for a in range(PASSES):
            nc.sync.dma_start(out=key_words[a][:].bitcast(I32), in_=ky_words[a].bitcast(I32))
        target = keep.tile([P, HALVES, TARGET_PITCH], F32, name="target")
        with nc.allow_non_contiguous_dma(reason="one target a partition and half"):
            nc.sync.dma_start(out=target[:, :, 0:1], in_=tg.rearrange("(h p) o -> p h o", h=HALVES))

        identity = keep.tile([P, P], F32, name="identity")
        make_identity(nc, identity[:])

        factor_ps = psum.tile([P, PACK, P], F32, name="factor_ps")
        for t in range(PACK):
            nc.tensor.transpose(factor_ps[:, t, :], fk_rows[:, t : P * PACK : PACK], identity[:])
        factor = keep.tile([P, PACK, PASSES], F32, name="factor")
        nc.vector.tensor_copy(out=factor[:], in_=factor_ps[:, :, FK_ROW : FK_ROW + PASSES])
        bi_columns_ps = psum.tile([P, P], F32, name="bi_columns_ps")
        nc.tensor.transpose(bi_columns_ps[:], bi_rows[:], identity[:])
        bi_columns = keep.tile([P, I // P], F32, name="bi_columns")
        nc.vector.tensor_copy(out=bi_columns[:], in_=bi_columns_ps[:, BI_ROW : BI_ROW + I // P])
        bias_ps = psum.tile([P, I], F32, name="bias_ps")
        for e in range(I // P):
            nc.tensor.transpose(
                bias_ps[:, e * P : (e + 1) * P], bi_columns[:, e : e + 1].to_broadcast([P, P]), identity[:])
        bias = keep.tile([P, I], F32, name="bias")
        nc.vector.tensor_copy(out=bias[:], in_=bias_ps[:])

        product_tiles = [keep.tile([P, PACK * J], F32, name=f"product_{a}", align_bytes=64) for a in range(PASSES)]
        product = [tile[:].rearrange("p (t c) -> p t c", t=PACK) for tile in product_tiles]
        picked_scales = [keep.tile([P, I], U8, name=f"picked_scales_{a}", align_bytes=64) for a in range(PASSES)]
        scores = [psum.tile([P, I], F32, name=f"scores_{h}") for h in range(HALVES)]

        whole = slice(0, J)
        halves = [slice(h * P, (h + 1) * P) for h in range(HALVES)]
        list_halves = [slice(h * P // ENTRIES_A_COLUMN, (h + 1) * P // ENTRIES_A_COLUMN) for h in range(HALVES)]
        third, last = PACK - 2, PACK - 1

        for a in range(PASSES):
            nc.vector.tensor_copy(out=picked_scales[a][:], in_=key_scales[:, a * V : (a + 1) * V].indirect(list_k[:]))

        entries = {}
        borrowed_plane = {(0, last): 0, (1, 0): third, (1, 1): last}
        for a in range(PASSES):
            for t in range(PACK):
                if (a, t) in borrowed_plane:
                    entries[a, t] = product[1][:, borrowed_plane[a, t], :]
                else:
                    tile = keep.tile([P, J], F32, name=f"entries_{a}_{t}", align_bytes=64)
                    entries[a, t] = tile[:]
                looked_up = xb_window[a, t].indirect(list_b[:])
                if a == 0 or t == 0:
                    nc.scalar.activation(out=entries[a, t], in_=looked_up, func=ACT.Copy)
                else:
                    nc.vector.tensor_copy(out=entries[a, t], in_=looked_up)

        last_scaled = [keep.tile([P, P], F32, name=f"last_scaled_{h}", align_bytes=64) for h in range(HALVES)]
        third_scaled = keep.tile([P, J], F32, name="third_scaled", align_bytes=64)
        nc.vector.tensor_scalar(
            out=third_scaled[:], in0=entries[1, third], scalar1=factor[:, third, 1:2], scalar2=None, op0=ALU.mult)
        for h in range(HALVES):
            nc.vector.tensor_scalar(
                out=last_scaled[h][:], in0=entries[1, last][:, halves[h]], scalar1=factor[:, last, 1:2], scalar2=None,
                op0=ALU.mult)

        def multiply_plane(a, t, tag):
            tokens = keep.tile([P, J], F32, name=f"tokens_{a}_{t}", tag=tag, align_bytes=64)
            nc.scalar.activation(out=tokens[:], in_=xf_window[a, t].indirect(list_f[:]), func=ACT.Copy)
            nc.vector.scalar_tensor_tensor(
                out=product[a][:, t, :], in0=tokens[:], scalar=factor[:, t, a : a + 1], in1=entries[a, t],
                op0=ALU.mult, op1=ALU.mult)

        def multiply_fused(t, cols, offsets, scaled):
            nc.vector.tensor_tensor(
                out=product[1][:, t, cols], in0=xf_window[1, t].indirect(offsets), in1=scaled, op=ALU.mult)

        def interleave(copy, a, cols, rounded):
            copy(
                out=rounded[:].rearrange("p (c i t) -> p c t i", i=RUN, t=PACK),
                in_=product[a][:, :, cols].rearrange("p t (c i) -> p c t i", i=RUN))

        def quantize(rounded, label):
            width = rounded.shape[1] // PACK
            codes = keep.tile([P, width], U32, name=f"codes_{label}", align_bytes=64)
            scales = keep.tile([P, width], U8, name=f"scales_{label}", align_bytes=64)
            nc.vector.quantize_mx(out=codes[:].bitcast(E5M2X4), scales=scales[:], in_=rounded[:])
            return codes, scales

        def product_pass(a, h, codes, scales, words):
            nc.tensor.matmul_mx(
                out=scores[h][:], lhsT=codes.bitcast(E5M2X4), lhsT_scale=scales,
                rhs=words[:].bitcast(E2M1X4), rhs_scale=picked_scales[a][:],
                start=(a == 0), stop=(a == PASSES - 1))

        multiply_plane(0, 0, "tokens_0_0")
        multiply_plane(0, 1, "tokens_0_1")
        multiply_plane(0, 2, "entries_0_0")
        multiply_plane(0, 3, "entries_0_1")
        first_rounded = keep.tile([P, J * PACK], BF16, name="first_rounded", align_bytes=64)
        interleave(nc.vector.tensor_copy, 0, whole, first_rounded)
        first_codes, first_scales = quantize(first_rounded, "first")

        multiply_plane(1, 0, "entries_0_2")
        multiply_plane(1, 1, "entries_0_1")
        multiply_fused(third, whole, list_f[:], third_scaled[:])
        for h in range(HALVES):
            multiply_fused(last, halves[h], list_f[:, list_halves[h]], last_scaled[h][:])
        rounded_0 = keep.tile([P, P * PACK], BF16, name="rounded_0", align_bytes=64)
        interleave(nc.scalar.copy, 1, halves[0], rounded_0)
        picked_words = [
            keep.tile([P, I], U16, name=f"picked_words_{a}", tag=f"last_scaled_{a}", align_bytes=64)
            for a in range(PASSES)]
        nc.vector.tensor_copy(out=picked_words[0][:], in_=key_words[0][:].indirect(list_k[:]))
        rounded_1 = keep.tile([P, P * PACK], BF16, name="rounded_1", tag="key_words_0", align_bytes=64)
        interleave(nc.scalar.copy, 1, halves[1], rounded_1)
        for h in range(HALVES):
            product_pass(0, h, first_codes[:, halves[h]], first_scales[:, halves[h]], picked_words[0])
        nc.vector.tensor_copy(out=picked_words[1][:], in_=key_words[1][:].indirect(list_k[:]))
        for h, rounded in enumerate((rounded_0, rounded_1)):
            codes, scales = quantize(rounded, f"second_{h}")
            product_pass(1, h, codes[:], scales[:], picked_words[1])

        excess = [keep.tile([P, I], F32, name=f"excess_{h}") for h in range(HALVES)]
        result = [keep.tile([P, I], F32, name=f"result_{h}") for h in range(HALVES)]
        for h in range(HALVES):
            nc.vector.scalar_tensor_tensor(
                out=excess[h][:], in0=scores[h][:], scalar=target[:, h, 0:1], in1=bias[:],
                op0=ALU.subtract, op1=ALU.add)
        for h in range(HALVES):
            nc.vector.scalar_tensor_tensor(
                out=result[h][:], in0=excess[h][:], scalar=0.0, in1=excess[h][:], op0=ALU.max, op1=ALU.mult)
            nc.sync.dma_start(out=out[halves[h], :], in_=result[h][:])
